import numpy as np
import ml_dtypes


def mxq(x, axis, fmt="e4m3"):
    dtype, down = {"e4m3": (ml_dtypes.float8_e4m3fn, 7), "e5m2": (ml_dtypes.float8_e5m2, 14)}[fmt]
    v = np.moveaxis(np.asarray(x, np.float32).astype(ml_dtypes.bfloat16).astype(np.float64), axis, -1)
    blocks = v.reshape(v.shape[:-1] + (-1, 32))
    amax = np.abs(blocks).max(-1, keepdims=True)
    byte = np.maximum(np.where(amax > 0, np.frexp(amax)[1] - 1 + 127, 0) - down, 1)
    scale = np.exp2(byte - 127.0)
    codes = (blocks / scale).astype(np.float32).astype(dtype).astype(np.float64)
    return np.moveaxis((codes * scale).reshape(v.shape), -1, axis)


WIDE = False


def mx_kscale(k):
    if not WIDE:
        return np.ones(k)
    levels = np.array([10, -10, 5, -5, 0])
    if k % 512:
        return np.exp2(np.random.permutation(np.resize(levels, k // 32))).repeat(32)
    a = np.empty((k // 512, 16))
    for p in range(k // 512):
        a[p, :8] = np.random.permutation(np.resize(levels, 8))
        for g in range(8):
            far = levels[np.abs(levels - a[p, g]) >= 10]
            a[p, g + 8] = far[np.random.randint(len(far))]
    return np.exp2(a.ravel()).repeat(32)


def f64(x):
    return np.asarray(x).astype(np.float64)


def striped(idx):
    return np.tile(np.asarray(idx).reshape(-1, 16).T, (8, 1)).astype(np.uint16)


def unstriped(offs):
    return offs[:16].T.reshape(-1).astype(np.int64)


E2M1 = np.array([0.0, 0.5, 1.0, 1.5, 2.0, 3.0, 4.0, 6.0, -0.0, -0.5, -1.0, -1.5, -2.0, -3.0, -4.0, -6.0])


def pack_weight(w, fmt):
    k, n = w.shape
    w = f64(np.asarray(w, np.float32).astype(ml_dtypes.bfloat16)).reshape(k // 32, 32, n)
    amax = np.abs(w).max(1)
    if fmt == "e4m3":
        byte = np.frexp(amax)[1] - 1 + 127 - 7
    else:
        mant, ex = np.frexp(amax / 6.0)
        byte = np.where(mant > 0.5, ex, ex - 1) + 127
    byte = np.clip(np.where(amax > 0, byte, 1), 1, 254)
    scaled = (w * np.exp2(127.0 - byte)[:, None, :]).reshape(k, n).astype(np.float32)
    by_word = np.ascontiguousarray(scaled.reshape(k // 512, 128, 4, n).transpose(0, 1, 3, 2))
    if fmt == "e4m3":
        words = by_word.astype(ml_dtypes.float8_e4m3fn).view(np.uint8)
    else:
        c = by_word.astype(ml_dtypes.float4_e2m1fn).view(np.uint8) & 0xF
        words = (c[..., 0::2] | (c[..., 1::2] << 4)).reshape(k // 512, 128, 2 * n)
    return np.ascontiguousarray(words), np.ascontiguousarray(byte.astype(np.uint8).reshape(k // 512, 16, n))


def unpack_weight(words, scales, fmt):
    g, _, n = scales.shape
    words = np.ascontiguousarray(words).reshape(g, 128, n, -1)
    if fmt == "e4m3":
        vals = words.view(ml_dtypes.float8_e4m3fn).astype(np.float64)
    else:
        nib = np.empty((g, 128, n, 4), np.uint8)
        nib[..., 0::2] = words & 0xF
        nib[..., 1::2] = words >> 4
        vals = E2M1[nib]
    vals = vals * np.repeat(np.exp2(scales.astype(np.float64) - 127.0), 8, axis=1)[..., None]
    return vals.transpose(0, 1, 3, 2).reshape(g * 512, n)


K, T, J, L, N, B, S = 512, 2048, 512, 512, 512, 64, 512


def setup_inputs():
    n = np.random.standard_normal
    idx = np.random.permutation(T)[:J]
    idx2 = np.random.permutation(S)[:B]
    fk = mx_kscale(K)
    fl = mx_kscale(L)
    wp = pack_weight(n((K, N)) * 1 / np.sqrt(K) * fk[:, None], "e2m1")
    sxp = pack_weight(n((L, J)) / fl[:, None], "e4m3")
    wsp = pack_weight(n((L, N)) * 1 / np.sqrt(L) * fl[:, None], "e2m1")
    return {
        "xf": (n((K, T))).astype(np.float32),
        "gv": (n((K, S))).astype(np.float32),
        "fk": (np.random.uniform(0.5, 2.0, (K, 1)) / fk[:, None]).astype(np.float32),
        "w_words": wp[0],
        "w_scales": wp[1],
        "sx_words": sxp[0],
        "sx_scales": sxp[1],
        "ws_words": wsp[0],
        "ws_scales": wsp[1],
        "offs": striped(idx),
        "offs2": striped(idx2),
    }


def reference(xf, gv, fk, w_words, w_scales, sx_words, sx_scales, ws_words, ws_scales, offs, offs2):
    idx = unstriped(offs)
    idx2 = unstriped(offs2)
    wu = unpack_weight(w_words, w_scales, "e2m1")
    sxu = unpack_weight(sx_words, sx_scales, "e4m3")
    wsu = unpack_weight(ws_words, ws_scales, "e2m1")
    g1 = f64(gv)[:, idx2]
    gr1 = np.repeat(g1, J // B, axis=1)
    xs = (f64(xf)[:, idx] + gr1) * f64(fk)
    xsq = mxq(xs, 0, "e4m3")
    y = wu.T @ xsq + wsu.T @ sxu
    return y

@@ -1,0 +1,162 @@
+from contextlib import ExitStack
+
+import concourse.mybir as mybir
+
+K, T, J, L, N, B, S = 512, 2048, 512, 512, 512, 64, 512
+FLOPS = 2 * N * J * (K + L)
+
+F32 = mybir.dt.float32
+BF16 = mybir.dt.bfloat16
+I32 = mybir.dt.int32
+U32 = mybir.dt.uint32
+U16 = mybir.dt.uint16
+U8 = mybir.dt.uint8
+FP8X4 = mybir.dt.float8_e4m3fn_x4
+FP4X4 = mybir.dt.float4_e2m1fn_x4
+ADD = mybir.AluOpType.add
+MULT = mybir.AluOpType.mult
+COPY = mybir.ActivationFunctionType.Copy
+
+P = 128
+PACK = 4
+GROUP = J // B
+CHUNK = 128
+CHUNKS = J // CHUNK
+LIST_COLS = CHUNK // 16
+ROW_TILES = N // P
+PAIR = 2
+SCALAR_CHUNKS = 2
+
+
+def tile_list_member_plus_picked_group_kernel(
+    tc, xf, gv, fk, w_words, w_scales, sx_words, sx_scales, ws_words, ws_scales, offs, offs2, out
+):
+    nc = tc.nc
+    with ExitStack() as ctx:
+        keep = ctx.enter_context(tc.tile_pool(name="keep", bufs=1))
+        psum = ctx.enter_context(tc.psum_pool(name="psum", bufs=1))
+
+        slots = keep.tile([P, J // 16], U16, name="slots")
+        groups = keep.tile([P, B // 16], U16, name="groups")
+        table = keep.tile([P, PACK * S], F32, name="table")
+        factor = keep.tile([P, PACK], F32, name="factor")
+        tokens = [keep.tile([P, T], F32, name="tokens%d" % t) for t in range(PACK)]
+        ws_codes = keep.tile([P, 2 * N], U8, name="ws_codes", align_bytes=64)
+        w_codes = keep.tile([P, 2 * N], U8, name="w_codes", align_bytes=64)
+        sx_first = keep.tile([P, CHUNK], U32, name="sx_first", align_bytes=64)
+        sx_rest = keep.tile([P, J - CHUNK], U32, name="sx_rest", align_bytes=64)
+        ws_plane = keep.tile([P, N], U8, name="ws_plane", align_bytes=64)
+        sx_plane = keep.tile([P, J], U8, name="sx_plane", align_bytes=64)
+        w_plane = keep.tile([P, N], U8, name="w_plane", align_bytes=64)
+
+        scale_loads = []
+        for plane, rows in ((ws_plane, ws_scales), (sx_plane, sx_scales), (w_plane, w_scales)):
+            nc.vector.memset(plane[:].bitcast(I32), 0)
+            for q in range(4):
+                scale_loads.append((plane[32 * q : 32 * q + 4, :].bitcast(I32), rows[0, 4 * q : 4 * q + 4, :].bitcast(I32)))
+
+        def load_scales(first, last):
+            for dst, src in scale_loads[first:last]:
+                nc.sync.dma_start(out=dst, in_=src)
+
+        xf_planes = xf.rearrange("(p t) c -> p t c", t=PACK)
+        sx_rows = sx_words[0].rearrange("p c r -> p (c r)").bitcast(I32)
+
+        nc.sync.dma_start(out=table[:], in_=gv.rearrange("(p t) s -> p (t s)", t=PACK))
+        nc.sync.dma_start(groups[:], offs2)
+        nc.sync.dma_start(slots[:], offs)
+        nc.sync.dma_start(out=tokens[0][:], in_=xf_planes[:, 0, :])
+        nc.sync.dma_start(out=factor[:], in_=fk.rearrange("(p t) o -> p (t o)", t=PACK))
+        load_scales(0, 3)
+        nc.sync.dma_start(out=tokens[1][:], in_=xf_planes[:, 1, :])
+        load_scales(3, 9)
+        nc.sync.dma_start(out=tokens[2][:], in_=xf_planes[:, 2, :])
+        load_scales(9, 12)
+        nc.sync.dma_start(out=tokens[3][:], in_=xf_planes[:, 3, :])
+        nc.sync.dma_start(out=ws_codes[:].bitcast(I32), in_=ws_words[0].bitcast(I32))
+        nc.sync.dma_start(out=sx_first[:].bitcast(I32), in_=sx_rows[:, 0:CHUNK])
+        nc.sync.dma_start(out=w_codes[:].bitcast(I32), in_=w_words[0].bitcast(I32))
+        nc.sync.dma_start(out=sx_rest[:].bitcast(I32), in_=sx_rows[:, CHUNK:J])
+
+        picked = keep.tile([P, PACK, B], F32, name="picked")
+        spread = [keep.tile([P, J], F32, name="spread%d" % t) for t in range(PACK)]
+        for t in range(PACK):
+            nc.vector.tensor_copy(picked[:, t, :], table[:, t * S : (t + 1) * S].indirect(groups[:]))
+            nc.scalar.copy(
+                spread[t][:].rearrange("p (b i) -> p b i", i=GROUP),
+                picked[:, t, :].unsqueeze(2).to_broadcast([P, B, GROUP]),
+            )
+
+        woven = [keep.tile([P, CHUNK, PACK], BF16, name="woven%d" % c, tag="woven%d" % c, align_bytes=64) for c in range(CHUNKS)]
+        codes = [keep.tile([P, CHUNK], U32, name="codes%d" % c, align_bytes=64) for c in range(CHUNKS)]
+        planes = [keep.tile([P, CHUNK], U8, name="plane%d" % c, align_bytes=64) for c in range(CHUNKS)]
+        sums = {}
+
+        def gather(t, c):
+            tag = "woven%d" % (c - 2) if t == PACK - 1 and c >= 2 else "sum%d_%d" % (t, c)
+            sums[t, c] = keep.tile([P, CHUNK], F32, name="sum%d_%d" % (t, c), tag=tag, align_bytes=64)
+            nc.vector.tensor_tensor(
+                sums[t, c][:],
+                tokens[t][:].indirect(slots[:, c * LIST_COLS : (c + 1) * LIST_COLS]),
+                spread[t][:, c * CHUNK : (c + 1) * CHUNK],
+                ADD,
+            )
+
+        def weave(t, c):
+            if t < 2 or c < SCALAR_CHUNKS:
+                nc.scalar.activation(woven[c][:, :, t], sums[t, c][:], COPY, scale=factor[:, t : t + 1])
+            else:
+                nc.vector.tensor_scalar(woven[c][:, :, t], sums[t, c][:], factor[:, t : t + 1], None, MULT)
+
+        def quantize(c):
+            nc.vector.quantize_mx(
+                out=codes[c][:].bitcast(FP8X4), scales=planes[c][:], in_=woven[c][:].rearrange("p j t -> p (j t)")
+            )
+
+        out_tiles = out.rearrange("(m p) j -> p m j", p=P)
+
+        def multiply(c):
+            cols = slice(c * CHUNK, (c + 1) * CHUNK)
+            sx_codes = sx_first[:] if c == 0 else sx_rest[:, (c - 1) * CHUNK : c * CHUNK]
+            banks = [psum.tile([P, PAIR, CHUNK], F32, name="bank%d_%d" % (c, h)) for h in range(ROW_TILES // PAIR)]
+            for m in range(ROW_TILES):
+                nc.tensor.matmul_mx(
+                    out=banks[m // PAIR][:, m % PAIR, :],
+                    lhsT=ws_codes[:, 2 * P * m : 2 * P * (m + 1)].bitcast(FP4X4),
+                    lhsT_scale=ws_plane[:, P * m : P * (m + 1)],
+                    rhs=sx_codes.bitcast(FP8X4),
+                    rhs_scale=sx_plane[:, cols],
+                    start=(m % PAIR == 0),
+                    stop=False,
+                )
+            for m in range(ROW_TILES):
+                nc.tensor.matmul_mx(
+                    out=banks[m // PAIR][:, m % PAIR, :],
+                    lhsT=w_codes[:, 2 * P * m : 2 * P * (m + 1)].bitcast(FP4X4),
+                    lhsT_scale=w_plane[:, P * m : P * (m + 1)],
+                    rhs=codes[c][:].bitcast(FP8X4),
+                    rhs_scale=planes[c][:],
+                    start=False,
+                    stop=(m % PAIR == PAIR - 1),
+                )
+            for h, bank in enumerate(banks):
+                result = keep.tile([P, PAIR, CHUNK], F32, name="result%d_%d" % (c, h))
+                if c == CHUNKS - 1 and h == 1:
+                    nc.vector.tensor_copy(result[:], bank[:])
+                else:
+                    nc.scalar.copy(result[:], bank[:])
+                nc.sync.dma_start(out=out_tiles[:, PAIR * h : PAIR * (h + 1), cols], in_=result[:])
+
+        for t in range(PACK - 1):
+            for c in range(CHUNKS):
+                gather(t, c)
+                weave(t, c)
+        last = PACK - 1
+        for c in range(CHUNKS + 1):
+            if c < CHUNKS:
+                gather(last, c)
+            if c >= 1:
+                quantize(c - 1)
+                multiply(c - 1)
+            if c < CHUNKS:
+                weave(last, c)

@@ -22,10 +22,10 @@ PACK = 4
 GROUP = J // B
 CHUNK = 128
 CHUNKS = J // CHUNK
-LIST_COLS = CHUNK // 16
 ROW_TILES = N // P
 PAIR = 2
 SCALAR_CHUNKS = 2
+HELD = 2
 
 
 def tile_list_member_plus_picked_group_kernel(
@@ -92,21 +92,36 @@ def tile_list_member_plus_picked_group_kernel(
         planes = [keep.tile([P, CHUNK], U8, name="plane%d" % c, align_bytes=64) for c in range(CHUNKS)]
         sums = {}
 
+        def pieces(t, c):
+            if t == PACK - 1 and c == 0:
+                return [(0, CHUNK // 2), (CHUNK // 2, CHUNK)]
+            return [(0, CHUNK)]
+
         def gather(t, c):
-            tag = "woven%d" % (c - 2) if t == PACK - 1 and c >= 2 else "sum%d_%d" % (t, c)
-            sums[t, c] = keep.tile([P, CHUNK], F32, name="sum%d_%d" % (t, c), tag=tag, align_bytes=64)
-            nc.vector.tensor_tensor(
-                sums[t, c][:],
-                tokens[t][:].indirect(slots[:, c * LIST_COLS : (c + 1) * LIST_COLS]),
-                spread[t][:, c * CHUNK : (c + 1) * CHUNK],
-                ADD,
-            )
+            if t == PACK - 1 and c >= HELD:
+                if c == HELD:
+                    sums["held"] = keep.tile(
+                        [P, CHUNKS - HELD, CHUNK], F32, name="held_sums", tag="woven0", align_bytes=64
+                    )
+                sums[t, c] = sums["held"][:, c - HELD, :]
+            else:
+                sums[t, c] = keep.tile([P, CHUNK], F32, name="sum%d_%d" % (t, c))
+            for lo, hi in pieces(t, c):
+                nc.vector.tensor_tensor(
+                    sums[t, c][:, lo:hi],
+                    tokens[t][:].indirect(slots[:, (c * CHUNK + lo) // 16 : (c * CHUNK + hi) // 16]),
+                    spread[t][:, c * CHUNK + lo : c * CHUNK + hi],
+                    ADD,
+                )
 
         def weave(t, c):
-            if t < 2 or c < SCALAR_CHUNKS:
-                nc.scalar.activation(woven[c][:, :, t], sums[t, c][:], COPY, scale=factor[:, t : t + 1])
-            else:
-                nc.vector.tensor_scalar(woven[c][:, :, t], sums[t, c][:], factor[:, t : t + 1], None, MULT)
+            for lo, hi in pieces(t, c):
+                if t < 2 or c < SCALAR_CHUNKS:
+                    nc.scalar.activation(woven[c][:, lo:hi, t], sums[t, c][:, lo:hi], COPY, scale=factor[:, t : t + 1])
+                else:
+                    nc.vector.tensor_scalar(
+                        woven[c][:, lo:hi, t], sums[t, c][:, lo:hi], factor[:, t : t + 1], None, MULT
+                    )
 
         def quantize(c):
             nc.vector.quantize_mx(
@@ -141,7 +156,7 @@ def tile_list_member_plus_picked_group_kernel(
                 )
             for h, bank in enumerate(banks):
                 result = keep.tile([P, PAIR, CHUNK], F32, name="result%d_%d" % (c, h))
-                if c == CHUNKS - 1 and h == 1:
+                if c >= 2 and h == 1:
                     nc.vector.tensor_copy(result[:], bank[:])
                 else:
                     nc.scalar.copy(result[:], bank[:])

@@ -24,7 +24,6 @@ CHUNK = 128
 CHUNKS = J // CHUNK
 ROW_TILES = N // P
 PAIR = 2
-SCALAR_CHUNKS = 2
 HELD = 2
 
 
@@ -62,20 +61,20 @@ def tile_list_member_plus_picked_group_kernel(
         xf_planes = xf.rearrange("(p t) c -> p t c", t=PACK)
         sx_rows = sx_words[0].rearrange("p c r -> p (c r)").bitcast(I32)
 
-        nc.sync.dma_start(out=table[:], in_=gv.rearrange("(p t) s -> p (t s)", t=PACK))
         nc.sync.dma_start(groups[:], offs2)
         nc.sync.dma_start(slots[:], offs)
+        nc.sync.dma_start(out=table[:], in_=gv.rearrange("(p t) s -> p (t s)", t=PACK))
         nc.sync.dma_start(out=tokens[0][:], in_=xf_planes[:, 0, :])
         nc.sync.dma_start(out=factor[:], in_=fk.rearrange("(p t) o -> p (t o)", t=PACK))
-        load_scales(0, 3)
+        load_scales(0, 4)
         nc.sync.dma_start(out=tokens[1][:], in_=xf_planes[:, 1, :])
-        load_scales(3, 9)
         nc.sync.dma_start(out=tokens[2][:], in_=xf_planes[:, 2, :])
-        load_scales(9, 12)
+        load_scales(4, 9)
         nc.sync.dma_start(out=tokens[3][:], in_=xf_planes[:, 3, :])
         nc.sync.dma_start(out=ws_codes[:].bitcast(I32), in_=ws_words[0].bitcast(I32))
         nc.sync.dma_start(out=sx_first[:].bitcast(I32), in_=sx_rows[:, 0:CHUNK])
         nc.sync.dma_start(out=w_codes[:].bitcast(I32), in_=w_words[0].bitcast(I32))
+        load_scales(9, 12)
         nc.sync.dma_start(out=sx_rest[:].bitcast(I32), in_=sx_rows[:, CHUNK:J])
 
         picked = keep.tile([P, PACK, B], F32, name="picked")
@@ -116,7 +115,7 @@ def tile_list_member_plus_picked_group_kernel(
 
         def weave(t, c):
             for lo, hi in pieces(t, c):
-                if t < 2 or c < SCALAR_CHUNKS:
+                if c < (HELD if t == PACK - 1 else CHUNKS - 1):
                     nc.scalar.activation(woven[c][:, lo:hi, t], sums[t, c][:, lo:hi], COPY, scale=factor[:, t : t + 1])
                 else:
                     nc.vector.tensor_scalar(

from contextlib import ExitStack

import concourse.mybir as mybir

K, T, J, L, N, B, S = 512, 2048, 512, 512, 512, 64, 512
FLOPS = 2 * N * J * (K + L)

F32 = mybir.dt.float32
BF16 = mybir.dt.bfloat16
I32 = mybir.dt.int32
U32 = mybir.dt.uint32
U16 = mybir.dt.uint16
U8 = mybir.dt.uint8
FP8X4 = mybir.dt.float8_e4m3fn_x4
FP4X4 = mybir.dt.float4_e2m1fn_x4
ADD = mybir.AluOpType.add
MULT = mybir.AluOpType.mult
COPY = mybir.ActivationFunctionType.Copy

P = 128
PACK = 4
GROUP = J // B
CHUNK = 128
CHUNKS = J // CHUNK
ROW_TILES = N // P
PAIR = 2
HELD = 2


def tile_list_member_plus_picked_group_kernel(
    tc, xf, gv, fk, w_words, w_scales, sx_words, sx_scales, ws_words, ws_scales, offs, offs2, out
):
    nc = tc.nc
    with ExitStack() as ctx:
        keep = ctx.enter_context(tc.tile_pool(name="keep", bufs=1))
        psum = ctx.enter_context(tc.psum_pool(name="psum", bufs=1))

        slots = keep.tile([P, J // 16], U16, name="slots")
        groups = keep.tile([P, B // 16], U16, name="groups")
        table = keep.tile([P, PACK * S], F32, name="table")
        factor = keep.tile([P, PACK], F32, name="factor")
        tokens = [keep.tile([P, T], F32, name="tokens%d" % t) for t in range(PACK)]
        ws_codes = keep.tile([P, 2 * N], U8, name="ws_codes", align_bytes=64)
        w_codes = keep.tile([P, 2 * N], U8, name="w_codes", align_bytes=64)
        sx_first = keep.tile([P, CHUNK], U32, name="sx_first", align_bytes=64)
        sx_rest = keep.tile([P, J - CHUNK], U32, name="sx_rest", align_bytes=64)
        ws_plane = keep.tile([P, N], U8, name="ws_plane", align_bytes=64)
        sx_plane = keep.tile([P, J], U8, name="sx_plane", align_bytes=64)
        w_plane = keep.tile([P, N], U8, name="w_plane", align_bytes=64)

        scale_loads = []
        for plane, rows in ((ws_plane, ws_scales), (sx_plane, sx_scales), (w_plane, w_scales)):
            nc.vector.memset(plane[:].bitcast(I32), 0)
            for q in range(4):
                scale_loads.append((plane[32 * q : 32 * q + 4, :].bitcast(I32), rows[0, 4 * q : 4 * q + 4, :].bitcast(I32)))

        def load_scales(first, last):
            for dst, src in scale_loads[first:last]:
                nc.sync.dma_start(out=dst, in_=src)

        xf_planes = xf.rearrange("(p t) c -> p t c", t=PACK)
        sx_rows = sx_words[0].rearrange("p c r -> p (c r)").bitcast(I32)

        nc.sync.dma_start(groups[:], offs2)
        nc.sync.dma_start(slots[:], offs)
        nc.sync.dma_start(out=table[:], in_=gv.rearrange("(p t) s -> p (t s)", t=PACK))
        nc.sync.dma_start(out=tokens[0][:], in_=xf_planes[:, 0, :])
        nc.sync.dma_start(out=factor[:], in_=fk.rearrange("(p t) o -> p (t o)", t=PACK))
        load_scales(0, 4)
        nc.sync.dma_start(out=tokens[1][:], in_=xf_planes[:, 1, :])
        nc.sync.dma_start(out=tokens[2][:], in_=xf_planes[:, 2, :])
        load_scales(4, 9)
        nc.sync.dma_start(out=tokens[3][:], in_=xf_planes[:, 3, :])
        nc.sync.dma_start(out=ws_codes[:].bitcast(I32), in_=ws_words[0].bitcast(I32))
        nc.sync.dma_start(out=sx_first[:].bitcast(I32), in_=sx_rows[:, 0:CHUNK])
        nc.sync.dma_start(out=w_codes[:].bitcast(I32), in_=w_words[0].bitcast(I32))
        load_scales(9, 12)
        nc.sync.dma_start(out=sx_rest[:].bitcast(I32), in_=sx_rows[:, CHUNK:J])

        picked = keep.tile([P, PACK, B], F32, name="picked")
        spread = [keep.tile([P, J], F32, name="spread%d" % t) for t in range(PACK)]
        for t in range(PACK):
            nc.vector.tensor_copy(picked[:, t, :], table[:, t * S : (t + 1) * S].indirect(groups[:]))
            nc.scalar.copy(
                spread[t][:].rearrange("p (b i) -> p b i", i=GROUP),
                picked[:, t, :].unsqueeze(2).to_broadcast([P, B, GROUP]),
            )

        woven = [keep.tile([P, CHUNK, PACK], BF16, name="woven%d" % c, tag="woven%d" % c, align_bytes=64) for c in range(CHUNKS)]
        codes = [keep.tile([P, CHUNK], U32, name="codes%d" % c, align_bytes=64) for c in range(CHUNKS)]
        planes = [keep.tile([P, CHUNK], U8, name="plane%d" % c, align_bytes=64) for c in range(CHUNKS)]
        sums = {}

        def pieces(t, c):
            if t == PACK - 1 and c == 0:
                return [(0, CHUNK // 2), (CHUNK // 2, CHUNK)]
            return [(0, CHUNK)]

        def gather(t, c):
            if t == PACK - 1 and c >= HELD:
                if c == HELD:
                    sums["held"] = keep.tile(
                        [P, CHUNKS - HELD, CHUNK], F32, name="held_sums", tag="woven0", align_bytes=64
                    )
                sums[t, c] = sums["held"][:, c - HELD, :]
            else:
                sums[t, c] = keep.tile([P, CHUNK], F32, name="sum%d_%d" % (t, c))
            for lo, hi in pieces(t, c):
                nc.vector.tensor_tensor(
                    sums[t, c][:, lo:hi],
                    tokens[t][:].indirect(slots[:, (c * CHUNK + lo) // 16 : (c * CHUNK + hi) // 16]),
                    spread[t][:, c * CHUNK + lo : c * CHUNK + hi],
                    ADD,
                )

        def weave(t, c):
            for lo, hi in pieces(t, c):
                if c < (HELD if t == PACK - 1 else CHUNKS - 1):
                    nc.scalar.activation(woven[c][:, lo:hi, t], sums[t, c][:, lo:hi], COPY, scale=factor[:, t : t + 1])
                else:
                    nc.vector.tensor_scalar(
                        woven[c][:, lo:hi, t], sums[t, c][:, lo:hi], factor[:, t : t + 1], None, MULT
                    )

        def quantize(c):
            nc.vector.quantize_mx(
                out=codes[c][:].bitcast(FP8X4), scales=planes[c][:], in_=woven[c][:].rearrange("p j t -> p (j t)")
            )

        out_tiles = out.rearrange("(m p) j -> p m j", p=P)

        def multiply(c):
            cols = slice(c * CHUNK, (c + 1) * CHUNK)
            sx_codes = sx_first[:] if c == 0 else sx_rest[:, (c - 1) * CHUNK : c * CHUNK]
            banks = [psum.tile([P, PAIR, CHUNK], F32, name="bank%d_%d" % (c, h)) for h in range(ROW_TILES // PAIR)]
            for m in range(ROW_TILES):
                nc.tensor.matmul_mx(
                    out=banks[m // PAIR][:, m % PAIR, :],
                    lhsT=ws_codes[:, 2 * P * m : 2 * P * (m + 1)].bitcast(FP4X4),
                    lhsT_scale=ws_plane[:, P * m : P * (m + 1)],
                    rhs=sx_codes.bitcast(FP8X4),
                    rhs_scale=sx_plane[:, cols],
                    start=(m % PAIR == 0),
                    stop=False,
                )
            for m in range(ROW_TILES):
                nc.tensor.matmul_mx(
                    out=banks[m // PAIR][:, m % PAIR, :],
                    lhsT=w_codes[:, 2 * P * m : 2 * P * (m + 1)].bitcast(FP4X4),
                    lhsT_scale=w_plane[:, P * m : P * (m + 1)],
                    rhs=codes[c][:].bitcast(FP8X4),
                    rhs_scale=planes[c][:],
                    start=False,
                    stop=(m % PAIR == PAIR - 1),
                )
            for h, bank in enumerate(banks):
                result = keep.tile([P, PAIR, CHUNK], F32, name="result%d_%d" % (c, h))
                if c >= 2 and h == 1:
                    nc.vector.tensor_copy(result[:], bank[:])
                else:
                    nc.scalar.copy(result[:], bank[:])
                nc.sync.dma_start(out=out_tiles[:, PAIR * h : PAIR * (h + 1), cols], in_=result[:])

        for t in range(PACK - 1):
            for c in range(CHUNKS):
                gather(t, c)
                weave(t, c)
        last = PACK - 1
        for c in range(CHUNKS + 1):
            if c < CHUNKS:
                gather(last, c)
            if c >= 1:
                quantize(c - 1)
                multiply(c - 1)
            if c < CHUNKS:
                weave(last, c)
